import numpy as np, ml_dtypes
CORES = [22,38,54,62,70,110,23,39,55,63,71,111]
N = 12
import mx_ref
NC, G, D = 384, 4, 64
C = np.float32(0.043)
BF = ml_dtypes.bfloat16
def cut(t, i, w=512):
    return t[:, w * i:w * i + w]
def tile(rs):
    return np.stack(rs, axis=2).reshape(128, -1).astype(BF)
def layer(w, X):
    out = []
    for i in range(G):
        for t in range(len(X)):
            p = mx_ref.matmul(mx_ref.quantize(cut(w, len(X) * i + t)), X[t])
            z = p if t == 0 else z + p
        out.append(z)
    return out
def act(Z):
    return [np.maximum(z, 0) * C for z in Z]
def setup_inputs(rng):
    def f(*shape):
        return mx_ref.flush((rng.standard_normal(shape, dtype=np.float32) * np.exp2(rng.integers(-2, 3, shape[:-1] + (1,)))).astype(BF))
    return {"x": f(N, 128, 4 * NC), "w1": np.broadcast_to(f(1, 128, G * 512), (N, 128, G * 512)).copy(), "wt": f(N, 128, 3 * 512)}
def setup_inputs_blocks(rng):
    d = setup_inputs(rng)
    for k in ("x", "wt"): d[k] = mx_ref.spread(d[k], rng, 2)
    return d
def setup_inputs_wide(rng):
    d = setup_inputs(rng)
    for k in ("wt",): d[k] = mx_ref.flush((d[k].astype(np.float32) * np.exp2(rng.integers(-6, 7, (N, 1, 1))).astype(np.float32)).astype(BF))
    return d
def setup_inputs_zeros(rng):
    d = setup_inputs(rng); v = d["x"].reshape(N, 128, -1, 4).copy()
    v[np.broadcast_to((rng.random((N, 1, v.shape[2], 1)) < 0.33), v.shape)] = 0
    d["x"] = v.reshape(d["x"].shape)
    return d
def reference(x, w1, wt):
    h = [tile(act(layer(w1[j], [mx_ref.quantize(x[j])]))) for j in range(N)]
    y = np.zeros((N, 128, NC), np.float32)
    for r in range(N):
        e = np.concatenate([h[(r - 1) % N][:, 4 * (NC - D):], h[r], h[(r + 1) % N][:, :4 * D]], axis=1)
        for t in range(3):
            p = mx_ref.matmul(mx_ref.quantize(cut(wt[r], t)), mx_ref.quantize(e[:, 4 * D * t:4 * D * t + 4 * NC]))
            y[r] = p if t == 0 else y[r] + p
    return {"y": y}

@@ -1,0 +1,182 @@
+from concourse.bass import DstId, RemoteDMATransfer
+from concourse.mybir import dt, AluOpType, ActivationFunctionType
+
+NT = 384
+D = 64
+SC = 0.043
+
+SCRATCH = {
+    "xt": ("sbuf", [128, 4 * NT], "bfloat16"),
+    "w1t": ("sbuf", [128, 4 * 512], "bfloat16"),
+    "wtt": ("sbuf", [128, 3 * 512], "bfloat16"),
+    "xq": ("sbuf", [128, NT + D], "float8_e4m3fn_x4"),
+    "xs": ("sbuf", [128, NT + D], "uint8"),
+    "w1q": ("sbuf", [128, 4 * 128], "float8_e4m3fn_x4"),
+    "w1s": ("sbuf", [128, 4 * 128], "uint8"),
+    "wtq": ("sbuf", [128, 3 * 128], "float8_e4m3fn_x4"),
+    "wts": ("sbuf", [128, 3 * 128], "uint8"),
+    "xhq": ("sbuf", [128, 2 * D], "float8_e4m3fn_x4"),
+    "xhs": ("sbuf", [128, 2 * D], "uint8"),
+    "ht": ("sbuf", [128, 4 * NT], "bfloat16"),
+    "hq": ("sbuf", [128, NT], "float8_e4m3fn_x4"),
+    "hs": ("sbuf", [128, NT], "uint8"),
+    "eht": ("sbuf", [128, 4 * 2 * D], "bfloat16"),
+    "ehq": ("sbuf", [128, 2 * D], "float8_e4m3fn_x4"),
+    "ehs": ("sbuf", [128, 2 * D], "uint8"),
+    "ps": ("psum", [128, 512 * 8], "float32"),
+    "ysb": ("sbuf", [128, NT], "float32"),
+}
+SEMAPHORES = (["ld_xe", "ld_xm", "ld_w1", "ld_wt", "q_xe", "q_x", "q_h", "q_eh", "halo", "left",
+               "a_0", "a_1", "a_2", "a_3", "a_3b", "yb", "ya", "yc", "c_b", "c_a", "c_c", "stored"]
+              + ["q_w%d" % i for i in range(4)] + ["q_t%d" % t for t in range(3)]
+              + ["z%d" % i for i in range(5)] + ["zh%d" % i for i in range(4)] + ["ah%d" % i for i in range(4)])
+HB = (5, 6, 7, 0)
+
+
+def split_mask(m):
+    bits = [b for b in range(32) if m >> b & 1]
+    half = len(bits) // 2
+    return sum(1 << b for b in bits[:half]), sum(1 << b for b in bits[half:])
+
+
+def rank_program(g, core, T, topo):
+    rank = T.rank_of(core)
+    if rank is None:
+        return
+    S = T.sem
+    V, P, A, Y = g.vector, g.tensor, g.scalar, g.sync
+    n = len(T.cores)
+    left, right = T.cores[(rank - 1) % n], T.cores[(rank + 1) % n]
+    u8 = dt.uint8
+    Relu, Copy = ActivationFunctionType.Relu, ActivationFunctionType.Copy
+
+    def bank(k, a, b):
+        return T.ps[:, 512 * k + a:512 * k + b]
+
+    def w1(i):
+        return T.w1q[:, 128 * i:128 * i + 128], T.w1s[:, 128 * i:128 * i + 128]
+
+    def wt(t):
+        return T.wtq[:, 128 * t:128 * t + 128], T.wts[:, 128 * t:128 * t + 128]
+
+    def own(a, b):
+        return T.hq[:, a:b], T.hs[:, a:b]
+
+    def mm(out, w, x, start, stop):
+        return P.matmul_mx(out, w[0], w[1], x[0], x[1], start, stop)
+
+    E = 4 * D
+
+    Y.dma_start(T.xt[:, E:2 * E], T.x[:, 0:E]).then_inc(S.ld_xe, 16)
+    A.dma_start(T.xt[:, 0:E], T.x[:, 5 * E:6 * E]).then_inc(S.ld_xe, 16)
+    Y.dma_start(T.xt[:, 2 * E:6 * E], T.x[:, E:5 * E]).then_inc(S.ld_xm, 16)
+    Y.dma_start(T.w1t[:], T.w1[:]).then_inc(S.ld_w1, 16)
+    Y.dma_start(T.wtt[:], T.wt[:]).then_inc(S.ld_wt, 16)
+
+    engines = topo.mask(core, left) & topo.mask(core, right)
+    m_l, m_r = split_mask(engines)
+    cnt = bin(engines).count("1")
+    rid_l, pid_l, _ = topo.addr(left)
+    rid_r, pid_r, _ = topo.addr(right)
+    to_l, to_r = DstId(rid=rid_l, pnc=pid_l), DstId(rid=rid_r, pnc=pid_r)
+    g.wait_ge(S.q_xe, 1)
+    g.remote_dma_fused([
+        RemoteDMATransfer(dst_ids=[to_r], dma_engine_mask=m_r, remote_sem=S.halo,
+                          src=T.xq[:, NT - D:NT].bitcast(u8), dst=T.xhq[:, 0:D].bitcast(u8)),
+        RemoteDMATransfer(dst_ids=[to_l], dma_engine_mask=m_l, remote_sem=S.halo,
+                          src=T.xq[:, NT:NT + D].bitcast(u8), dst=T.xhq[:, D:2 * D].bitcast(u8)),
+    ], local_sem=S.left)
+    g.remote_dma_fused([
+        RemoteDMATransfer(dst_ids=[to_r], dma_engine_mask=m_r, remote_sem=S.halo,
+                          src=T.xs[:, NT - D:NT], dst=T.xhs[:, 0:D]),
+        RemoteDMATransfer(dst_ids=[to_l], dma_engine_mask=m_l, remote_sem=S.halo,
+                          src=T.xs[:, NT:NT + D], dst=T.xhs[:, D:2 * D]),
+    ], local_sem=S.left)
+    g.wait_ge(S.left, 2 * cnt)
+
+    def act_s(out, zin, sem):
+        A.activation(out, zin, Relu, scale=SC).then_inc(sem, 1)
+
+    def act_v(out, zin, sem):
+        V.tensor_scalar(out, zin, 0.0, SC, AluOpType.max, AluOpType.mult).then_inc(sem, 1)
+
+    def h_cols(b, a, e):
+        return T.ht[:, 4 * a + b:4 * e:4]
+
+    def eh_cols(b):
+        return T.eht[:, b:8 * D:4]
+
+    V.wait_ge(S.ld_xe, 32)
+    V.quantize_mx(T.xq[:, NT - D:NT + D], T.xs[:, NT - D:NT + D], T.xt[:, 0:2 * E]).then_inc(S.q_xe, 1)
+    V.wait_ge(S.ld_xm, 16)
+    V.quantize_mx(T.xq[:, 0:NT - D], T.xs[:, 0:NT - D], T.xt[:, E:6 * E]).then_inc(S.q_x, 1)
+    V.wait_ge(S.ld_w1, 16)
+    for i in range(4):
+        q, s = w1(i)
+        V.quantize_mx(q, s, T.w1t[:, 512 * i:512 * i + 512]).then_inc(S["q_w%d" % i], 1)
+    V.wait_ge(S.z2, 1)
+    act_v(h_cols(2, 0, NT), bank(2, 0, NT), S.a_2)
+    V.wait_ge(S.z4, 1)
+    act_v(h_cols(3, NT // 2, NT), bank(4, 0, NT // 2), S.a_3b)
+    for s in ("a_0", "a_1", "a_2", "a_3", "a_3b"):
+        V.wait_ge(S[s], 1)
+    V.quantize_mx(T.hq[:], T.hs[:], T.ht[:]).then_inc(S.q_h, 1)
+    V.wait_ge(S.ld_wt, 16)
+    for t in (1, 0, 2):
+        q, s = wt(t)
+        V.quantize_mx(q, s, T.wtt[:, 512 * t:512 * t + 512]).then_inc(S["q_t%d" % t], 1)
+    for b in (1, 3):
+        V.wait_ge(S["zh%d" % b], 1)
+        act_v(eh_cols(b), bank(HB[b], 0, 2 * D), S["ah%d" % b])
+    for b in range(4):
+        V.wait_ge(S["ah%d" % b], 1)
+    V.quantize_mx(T.ehq[:], T.ehs[:], T.eht[:]).then_inc(S.q_eh, 1)
+    V.wait_ge(S.ya, 1)
+    V.tensor_copy(T.ysb[:, 0:D], bank(2, 0, D)).then_inc(S.c_a, 1)
+
+    P.wait_ge(S.q_xe, 1)
+    P.wait_ge(S.q_x, 1)
+    for i in range(3):
+        P.wait_ge(S["q_w%d" % i], 1)
+        mm(bank(i, 0, NT), w1(i), (T.xq[:, 0:NT], T.xs[:, 0:NT]), True, True).then_inc(S["z%d" % i], 1)
+    P.wait_ge(S.q_w3, 1)
+    for k in range(2):
+        a, e = k * NT // 2, (k + 1) * NT // 2
+        mm(bank(3 + k, 0, NT // 2), w1(3), (T.xq[:, a:e], T.xs[:, a:e]), True, True).then_inc(S["z%d" % (3 + k)], 1)
+    P.wait_ge(S.q_h, 1)
+    for k, t in enumerate((1, 0, 2)):
+        P.wait_ge(S["q_t%d" % t], 1)
+        r = mm(bank(1, 0, NT - 2 * D), wt(t), own(D * t, D * t + NT - 2 * D), k == 0, k == 2)
+    r.then_inc(S.yb, 1)
+    mm(bank(2, 0, 2 * D), wt(1), own(0, 2 * D), True, False)
+    mm(bank(2, 0, 2 * D), wt(2), own(D, 3 * D), False, False)
+    P.wait_ge(S.halo, 2 * cnt)
+    for b in range(4):
+        mm(bank(HB[b], 0, 2 * D), w1(b), (T.xhq[:], T.xhs[:]), True, True).then_inc(S["zh%d" % b], 1)
+    mm(bank(3, 0, 2 * D), wt(1), own(NT - 2 * D, NT), True, False)
+    mm(bank(3, 0, 2 * D), wt(0), own(NT - 3 * D, NT - D), False, False)
+    P.wait_ge(S.q_eh, 1)
+    edge = (T.ehq[:], T.ehs[:])
+    mm(bank(2, 0, 2 * D), wt(0), edge, False, True).then_inc(S.ya, 1)
+    mm(bank(3, 0, 2 * D), wt(2), edge, False, True).then_inc(S.yc, 1)
+
+    for i in range(2):
+        A.wait_ge(S["z%d" % i], 1)
+        act_s(h_cols(i, 0, NT), bank(i, 0, NT), S["a_%d" % i])
+    A.wait_ge(S.z3, 1)
+    act_s(h_cols(3, 0, NT // 2), bank(3, 0, NT // 2), S.a_3)
+    A.wait_ge(S.yb, 1)
+    A.activation(T.ysb[:, D:NT - D], bank(1, 0, NT - 2 * D), Copy).then_inc(S.c_b, 1)
+    for b in (0, 2):
+        A.wait_ge(S["zh%d" % b], 1)
+        act_s(eh_cols(b), bank(HB[b], 0, 2 * D), S["ah%d" % b])
+    A.wait_ge(S.yc, 1)
+    A.activation(T.ysb[:, NT - D:NT], bank(3, D, 2 * D), Copy).then_inc(S.c_c, 1)
+    A.wait_ge(S.c_c, 1)
+    A.dma_start(T.y[:, NT - D:NT], T.ysb[:, NT - D:NT]).then_inc(S.stored, 16)
+
+    Y.wait_ge(S.c_b, 1)
+    Y.dma_start(T.y[:, D:NT - D], T.ysb[:, D:NT - D]).then_inc(S.stored, 16)
+    Y.wait_ge(S.c_a, 1)
+    Y.dma_start(T.y[:, 0:D], T.ysb[:, 0:D]).then_inc(S.stored, 16)
+    Y.wait_ge(S.stored, 48)

@@ -3,40 +3,34 @@ from concourse.mybir import dt, AluOpType, ActivationFunctionType
 
 NT = 384
 D = 64
+E = 4 * D
 SC = 0.043
 
 SCRATCH = {
-    "xt": ("sbuf", [128, 4 * NT], "bfloat16"),
+    "xt": ("sbuf", [128, 6 * E], "bfloat16"),
     "w1t": ("sbuf", [128, 4 * 512], "bfloat16"),
     "wtt": ("sbuf", [128, 3 * 512], "bfloat16"),
-    "xq": ("sbuf", [128, NT + D], "float8_e4m3fn_x4"),
-    "xs": ("sbuf", [128, NT + D], "uint8"),
+    "xq": ("sbuf", [128, 7 * D], "float8_e4m3fn_x4"),
+    "xs": ("sbuf", [128, 7 * D], "uint8"),
     "w1q": ("sbuf", [128, 4 * 128], "float8_e4m3fn_x4"),
     "w1s": ("sbuf", [128, 4 * 128], "uint8"),
     "wtq": ("sbuf", [128, 3 * 128], "float8_e4m3fn_x4"),
     "wts": ("sbuf", [128, 3 * 128], "uint8"),
-    "xhq": ("sbuf", [128, 2 * D], "float8_e4m3fn_x4"),
-    "xhs": ("sbuf", [128, 2 * D], "uint8"),
-    "ht": ("sbuf", [128, 4 * NT], "bfloat16"),
-    "hq": ("sbuf", [128, NT], "float8_e4m3fn_x4"),
-    "hs": ("sbuf", [128, NT], "uint8"),
-    "eht": ("sbuf", [128, 4 * 2 * D], "bfloat16"),
-    "ehq": ("sbuf", [128, 2 * D], "float8_e4m3fn_x4"),
-    "ehs": ("sbuf", [128, 2 * D], "uint8"),
+    "ht": ("sbuf", [128, 6 * E], "bfloat16"),
+    "hq": ("sbuf", [128, 8 * D], "float8_e4m3fn_x4"),
+    "hs": ("sbuf", [128, 8 * D], "uint8"),
+    "rt": ("sbuf", [128, 2 * E], "bfloat16"),
+    "rq": ("sbuf", [128, 2 * D], "float8_e4m3fn_x4"),
+    "rs": ("sbuf", [128, 2 * D], "uint8"),
     "ps": ("psum", [128, 512 * 8], "float32"),
     "ysb": ("sbuf", [128, NT], "float32"),
 }
-SEMAPHORES = (["ld_xe", "ld_xm", "ld_w1", "ld_wt", "q_xe", "q_x", "q_h", "q_eh", "halo", "left",
-               "a_0", "a_1", "a_2", "a_3", "a_3b", "yb", "ya", "yc", "c_b", "c_a", "c_c", "stored"]
+SEMAPHORES = (["ld_xe", "ld_xm", "ld_wa", "ld_wb", "ld_ta", "ld_tb", "q_xe", "q_xm", "q_he", "q_hm", "q_hr",
+               "halo_r", "halo_l", "left", "ya", "yb", "yc", "c_a", "c_b", "c_c", "stored"]
               + ["q_w%d" % i for i in range(4)] + ["q_t%d" % t for t in range(3)]
-              + ["z%d" % i for i in range(5)] + ["zh%d" % i for i in range(4)] + ["ah%d" % i for i in range(4)])
-HB = (5, 6, 7, 0)
-
-
-def split_mask(m):
-    bits = [b for b in range(32) if m >> b & 1]
-    half = len(bits) // 2
-    return sum(1 << b for b in bits[:half]), sum(1 << b for b in bits[half:])
+              + [k + "%d" % b for k in ("ze", "zm", "zr", "ae", "am", "ar") for b in range(4)])
+BE, BM, BR = (0, 1, 2, 3), (4, 5, 6, 7), (0, 1, 2, 3)
+BA, BB, BC = 4, 5, 6
 
 
 def rank_program(g, core, T, topo):
@@ -59,124 +53,130 @@ def rank_program(g, core, T, topo):
     def wt(t):
         return T.wtq[:, 128 * t:128 * t + 128], T.wts[:, 128 * t:128 * t + 128]
 
-    def own(a, b):
-        return T.hq[:, a:b], T.hs[:, a:b]
+    def xb(a, b):
+        return T.xq[:, D * a:D * b], T.xs[:, D * a:D * b]
+
+    def hb(a, b):
+        return T.hq[:, D * a:D * b], T.hs[:, D * a:D * b]
 
     def mm(out, w, x, start, stop):
         return P.matmul_mx(out, w[0], w[1], x[0], x[1], start, stop)
 
-    E = 4 * D
-
     Y.dma_start(T.xt[:, E:2 * E], T.x[:, 0:E]).then_inc(S.ld_xe, 16)
     A.dma_start(T.xt[:, 0:E], T.x[:, 5 * E:6 * E]).then_inc(S.ld_xe, 16)
+    Y.dma_start(T.w1t[:, 0:1024], T.w1[:, 0:1024]).then_inc(S.ld_wa, 16)
+    Y.dma_start(T.w1t[:, 1024:2048], T.w1[:, 1024:2048]).then_inc(S.ld_wb, 16)
     Y.dma_start(T.xt[:, 2 * E:6 * E], T.x[:, E:5 * E]).then_inc(S.ld_xm, 16)
-    Y.dma_start(T.w1t[:], T.w1[:]).then_inc(S.ld_w1, 16)
-    Y.dma_start(T.wtt[:], T.wt[:]).then_inc(S.ld_wt, 16)
+    Y.dma_start(T.wtt[:, 0:1024], T.wt[:, 0:1024]).then_inc(S.ld_ta, 16)
+    Y.dma_start(T.wtt[:, 1024:1536], T.wt[:, 1024:1536]).then_inc(S.ld_tb, 16)
 
-    engines = topo.mask(core, left) & topo.mask(core, right)
-    m_l, m_r = split_mask(engines)
-    cnt = bin(engines).count("1")
-    rid_l, pid_l, _ = topo.addr(left)
-    rid_r, pid_r, _ = topo.addr(right)
-    to_l, to_r = DstId(rid=rid_l, pnc=pid_l), DstId(rid=rid_r, pnc=pid_r)
+    def send(dst, remote_sem, cq, ps, a, b):
+        rid, pid, _ = topo.addr(dst)
+        m = topo.mask(core, dst)
+        for o, i in ((cq[:, D * b:D * b + D].bitcast(u8), cq[:, D * a:D * a + D].bitcast(u8)),
+                     (ps[:, D * b:D * b + D], ps[:, D * a:D * a + D])):
+            g.remote_dma(out_ap=o, in_ap=i, remote_sem=remote_sem, local_sem=S.left, pid=pid, routing_id=rid,
+                         dma_engine_mask=m)
+        return 2 * bin(m).count("1")
+
     g.wait_ge(S.q_xe, 1)
-    g.remote_dma_fused([
-        RemoteDMATransfer(dst_ids=[to_r], dma_engine_mask=m_r, remote_sem=S.halo,
-                          src=T.xq[:, NT - D:NT].bitcast(u8), dst=T.xhq[:, 0:D].bitcast(u8)),
-        RemoteDMATransfer(dst_ids=[to_l], dma_engine_mask=m_l, remote_sem=S.halo,
-                          src=T.xq[:, NT:NT + D].bitcast(u8), dst=T.xhq[:, D:2 * D].bitcast(u8)),
-    ], local_sem=S.left)
-    g.remote_dma_fused([
-        RemoteDMATransfer(dst_ids=[to_r], dma_engine_mask=m_r, remote_sem=S.halo,
-                          src=T.xs[:, NT - D:NT], dst=T.xhs[:, 0:D]),
-        RemoteDMATransfer(dst_ids=[to_l], dma_engine_mask=m_l, remote_sem=S.halo,
-                          src=T.xs[:, NT:NT + D], dst=T.xhs[:, D:2 * D]),
-    ], local_sem=S.left)
-    g.wait_ge(S.left, 2 * cnt)
+    sent = send(left, S.halo_r, T.xq, T.xs, 5, 6)
+    g.wait_ge(S.q_he, 1)
+    sent += send(right, S.halo_l, T.hq, T.hs, 6, 0)
+    g.wait_ge(S.left, sent)
+    from_r = 2 * bin(topo.mask(right, core)).count("1")
+    from_l = 2 * bin(topo.mask(left, core)).count("1")
 
-    def act_s(out, zin, sem):
-        A.activation(out, zin, Relu, scale=SC).then_inc(sem, 1)
+    def to_tile(q, kind, b):
+        out, zin = {"e": (T.ht[:, b:2 * E:4], bank(BE[b], 0, 2 * D)),
+                    "m": (T.ht[:, 2 * E + b:6 * E:4], bank(BM[b], 0, 4 * D)),
+                    "r": (T.rt[:, b:2 * E:4], bank(BR[b], 0, 2 * D))}[kind]
+        q.wait_ge(S["z%s%d" % (kind, b)], 1)
+        if q is V:
+            r = V.tensor_scalar(out, zin, 0.0, SC, AluOpType.max, AluOpType.mult)
+        else:
+            r = A.activation(out, zin, Relu, scale=SC)
+        r.then_inc(S["a%s%d" % (kind, b)], 1)
 
-    def act_v(out, zin, sem):
-        V.tensor_scalar(out, zin, 0.0, SC, AluOpType.max, AluOpType.mult).then_inc(sem, 1)
+    def wait_tile(kind):
+        for b in range(4):
+            V.wait_ge(S["a%s%d" % (kind, b)], 1)
 
-    def h_cols(b, a, e):
-        return T.ht[:, 4 * a + b:4 * e:4]
-
-    def eh_cols(b):
-        return T.eht[:, b:8 * D:4]
-
-    V.wait_ge(S.ld_xe, 32)
-    V.quantize_mx(T.xq[:, NT - D:NT + D], T.xs[:, NT - D:NT + D], T.xt[:, 0:2 * E]).then_inc(S.q_xe, 1)
-    V.wait_ge(S.ld_xm, 16)
-    V.quantize_mx(T.xq[:, 0:NT - D], T.xs[:, 0:NT - D], T.xt[:, E:6 * E]).then_inc(S.q_x, 1)
-    V.wait_ge(S.ld_w1, 16)
-    for i in range(4):
-        q, s = w1(i)
-        V.quantize_mx(q, s, T.w1t[:, 512 * i:512 * i + 512]).then_inc(S["q_w%d" % i], 1)
-    V.wait_ge(S.z2, 1)
-    act_v(h_cols(2, 0, NT), bank(2, 0, NT), S.a_2)
-    V.wait_ge(S.z4, 1)
-    act_v(h_cols(3, NT // 2, NT), bank(4, 0, NT // 2), S.a_3b)
-    for s in ("a_0", "a_1", "a_2", "a_3", "a_3b"):
-        V.wait_ge(S[s], 1)
-    V.quantize_mx(T.hq[:], T.hs[:], T.ht[:]).then_inc(S.q_h, 1)
-    V.wait_ge(S.ld_wt, 16)
-    for t in (1, 0, 2):
+    def q_wt(t):
         q, s = wt(t)
         V.quantize_mx(q, s, T.wtt[:, 512 * t:512 * t + 512]).then_inc(S["q_t%d" % t], 1)
-    for b in (1, 3):
-        V.wait_ge(S["zh%d" % b], 1)
-        act_v(eh_cols(b), bank(HB[b], 0, 2 * D), S["ah%d" % b])
-    for b in range(4):
-        V.wait_ge(S["ah%d" % b], 1)
-    V.quantize_mx(T.ehq[:], T.ehs[:], T.eht[:]).then_inc(S.q_eh, 1)
-    V.wait_ge(S.ya, 1)
-    V.tensor_copy(T.ysb[:, 0:D], bank(2, 0, D)).then_inc(S.c_a, 1)
+
+    V.wait_ge(S.ld_xe, 32)
+    V.quantize_mx(T.xq[:, 4 * D:6 * D], T.xs[:, 4 * D:6 * D], T.xt[:, 0:2 * E]).then_inc(S.q_xe, 1)
+    for i in range(4):
+        if i == 0:
+            V.wait_ge(S.ld_wa, 16)
+        if i == 2:
+            V.wait_ge(S.ld_wb, 16)
+        q, s = w1(i)
+        V.quantize_mx(q, s, T.w1t[:, 512 * i:512 * i + 512]).then_inc(S["q_w%d" % i], 1)
+    V.wait_ge(S.ld_xm, 16)
+    V.quantize_mx(T.xq[:, 0:4 * D], T.xs[:, 0:4 * D], T.xt[:, 2 * E:6 * E]).then_inc(S.q_xm, 1)
+    wait_tile("e")
+    V.quantize_mx(T.hq[:, 6 * D:8 * D], T.hs[:, 6 * D:8 * D], T.ht[:, 0:2 * E]).then_inc(S.q_he, 1)
+    to_tile(V, "m", 1)
+    V.wait_ge(S.ld_ta, 16)
+    q_wt(1)
+    to_tile(V, "m", 3)
+    wait_tile("m")
+    V.quantize_mx(T.hq[:, D:6 * D], T.hs[:, D:6 * D], T.ht[:, E:6 * E]).then_inc(S.q_hm, 1)
+    q_wt(0)
+    V.wait_ge(S.ld_tb, 16)
+    q_wt(2)
+    V.wait_ge(S.yb, 1)
+    V.tensor_copy(T.ysb[:, 2 * D:5 * D], bank(BB, 0, 3 * D)).then_inc(S.c_b, 1)
+    to_tile(V, "r", 1)
+    to_tile(V, "r", 3)
+    wait_tile("r")
+    V.quantize_mx(T.rq[:], T.rs[:], T.rt[:]).then_inc(S.q_hr, 1)
+    V.wait_ge(S.yc, 1)
+    V.tensor_copy(T.ysb[:, 5 * D:6 * D], bank(BC, D, 2 * D)).then_inc(S.c_c, 1)
 
     P.wait_ge(S.q_xe, 1)
-    P.wait_ge(S.q_x, 1)
-    for i in range(3):
-        P.wait_ge(S["q_w%d" % i], 1)
-        mm(bank(i, 0, NT), w1(i), (T.xq[:, 0:NT], T.xs[:, 0:NT]), True, True).then_inc(S["z%d" % i], 1)
-    P.wait_ge(S.q_w3, 1)
-    for k in range(2):
-        a, e = k * NT // 2, (k + 1) * NT // 2
-        mm(bank(3 + k, 0, NT // 2), w1(3), (T.xq[:, a:e], T.xs[:, a:e]), True, True).then_inc(S["z%d" % (3 + k)], 1)
-    P.wait_ge(S.q_h, 1)
-    for k, t in enumerate((1, 0, 2)):
-        P.wait_ge(S["q_t%d" % t], 1)
-        r = mm(bank(1, 0, NT - 2 * D), wt(t), own(D * t, D * t + NT - 2 * D), k == 0, k == 2)
-    r.then_inc(S.yb, 1)
-    mm(bank(2, 0, 2 * D), wt(1), own(0, 2 * D), True, False)
-    mm(bank(2, 0, 2 * D), wt(2), own(D, 3 * D), False, False)
-    P.wait_ge(S.halo, 2 * cnt)
     for b in range(4):
-        mm(bank(HB[b], 0, 2 * D), w1(b), (T.xhq[:], T.xhs[:]), True, True).then_inc(S["zh%d" % b], 1)
-    mm(bank(3, 0, 2 * D), wt(1), own(NT - 2 * D, NT), True, False)
-    mm(bank(3, 0, 2 * D), wt(0), own(NT - 3 * D, NT - D), False, False)
-    P.wait_ge(S.q_eh, 1)
-    edge = (T.ehq[:], T.ehs[:])
-    mm(bank(2, 0, 2 * D), wt(0), edge, False, True).then_inc(S.ya, 1)
-    mm(bank(3, 0, 2 * D), wt(2), edge, False, True).then_inc(S.yc, 1)
+        P.wait_ge(S["q_w%d" % b], 1)
+        mm(bank(BE[b], 0, 2 * D), w1(b), xb(4, 6), True, True).then_inc(S["ze%d" % b], 1)
+    P.wait_ge(S.q_xm, 1)
+    for b in (1, 0, 2, 3):
+        mm(bank(BM[b], 0, 4 * D), w1(b), xb(0, 4), True, True).then_inc(S["zm%d" % b], 1)
+    P.wait_ge(S.q_he, 1)
+    P.wait_ge(S.q_hm, 1)
+    P.wait_ge(S.q_t1, 1)
+    mm(bank(BA, 0, 2 * D), wt(1), hb(1, 3), True, False)
+    mm(bank(BB, 0, 3 * D), wt(1), hb(3, 6), True, False)
+    P.wait_ge(S.q_t0, 1)
+    mm(bank(BB, 0, 3 * D), wt(0), hb(2, 5), False, False)
+    P.wait_ge(S.q_t2, 1)
+    mm(bank(BB, 0, 3 * D), wt(2), hb(4, 7), False, True).then_inc(S.yb, 1)
+    P.wait_ge(S.halo_r, from_r)
+    for b in range(4):
+        mm(bank(BR[b], 0, 2 * D), w1(b), xb(5, 7), True, True).then_inc(S["zr%d" % b], 1)
+    mm(bank(BA, 0, 2 * D), wt(2), hb(2, 4), False, False)
+    mm(bank(BC, 0, 2 * D), wt(0), hb(4, 6), True, False)
+    P.wait_ge(S.halo_l, from_l)
+    mm(bank(BA, 0, 2 * D), wt(0), hb(0, 2), False, True).then_inc(S.ya, 1)
+    mm(bank(BC, 0, 2 * D), wt(1), hb(5, 7), False, False)
+    P.wait_ge(S.q_hr, 1)
+    mm(bank(BC, 0, 2 * D), wt(2), (T.rq[:], T.rs[:]), False, True).then_inc(S.yc, 1)
 
-    for i in range(2):
-        A.wait_ge(S["z%d" % i], 1)
-        act_s(h_cols(i, 0, NT), bank(i, 0, NT), S["a_%d" % i])
-    A.wait_ge(S.z3, 1)
-    act_s(h_cols(3, 0, NT // 2), bank(3, 0, NT // 2), S.a_3)
-    A.wait_ge(S.yb, 1)
-    A.activation(T.ysb[:, D:NT - D], bank(1, 0, NT - 2 * D), Copy).then_inc(S.c_b, 1)
+    for b in range(4):
+        to_tile(A, "e", b)
     for b in (0, 2):
-        A.wait_ge(S["zh%d" % b], 1)
-        act_s(eh_cols(b), bank(HB[b], 0, 2 * D), S["ah%d" % b])
-    A.wait_ge(S.yc, 1)
-    A.activation(T.ysb[:, NT - D:NT], bank(3, D, 2 * D), Copy).then_inc(S.c_c, 1)
-    A.wait_ge(S.c_c, 1)
-    A.dma_start(T.y[:, NT - D:NT], T.ysb[:, NT - D:NT]).then_inc(S.stored, 16)
+        to_tile(A, "m", b)
+    for b in (0, 2):
+        to_tile(A, "r", b)
+    A.wait_ge(S.ya, 1)
+    A.activation(T.ysb[:, 0:2 * D], bank(BA, 0, 2 * D), Copy).then_inc(S.c_a, 1)
+    A.wait_ge(S.c_a, 1)
+    A.dma_start(T.y[:, 0:2 * D], T.ysb[:, 0:2 * D]).then_inc(S.stored, 16)
 
     Y.wait_ge(S.c_b, 1)
-    Y.dma_start(T.y[:, D:NT - D], T.ysb[:, D:NT - D]).then_inc(S.stored, 16)
-    Y.wait_ge(S.c_a, 1)
-    Y.dma_start(T.y[:, 0:D], T.ysb[:, 0:D]).then_inc(S.stored, 16)
+    Y.dma_start(T.y[:, 2 * D:5 * D], T.ysb[:, 2 * D:5 * D]).then_inc(S.stored, 16)
+    Y.wait_ge(S.c_c, 1)
+    Y.dma_start(T.y[:, 5 * D:6 * D], T.ysb[:, 5 * D:6 * D]).then_inc(S.stored, 16)
     Y.wait_ge(S.stored, 48)

from concourse.bass import DstId, RemoteDMATransfer
from concourse.mybir import dt, AluOpType, ActivationFunctionType

NT = 384
D = 64
E = 4 * D
SC = 0.043

SCRATCH = {
    "xt": ("sbuf", [128, 6 * E], "bfloat16"),
    "w1t": ("sbuf", [128, 4 * 512], "bfloat16"),
    "wtt": ("sbuf", [128, 3 * 512], "bfloat16"),
    "xq": ("sbuf", [128, 7 * D], "float8_e4m3fn_x4"),
    "xs": ("sbuf", [128, 7 * D], "uint8"),
    "w1q": ("sbuf", [128, 4 * 128], "float8_e4m3fn_x4"),
    "w1s": ("sbuf", [128, 4 * 128], "uint8"),
    "wtq": ("sbuf", [128, 3 * 128], "float8_e4m3fn_x4"),
    "wts": ("sbuf", [128, 3 * 128], "uint8"),
    "ht": ("sbuf", [128, 6 * E], "bfloat16"),
    "hq": ("sbuf", [128, 8 * D], "float8_e4m3fn_x4"),
    "hs": ("sbuf", [128, 8 * D], "uint8"),
    "rt": ("sbuf", [128, 2 * E], "bfloat16"),
    "rq": ("sbuf", [128, 2 * D], "float8_e4m3fn_x4"),
    "rs": ("sbuf", [128, 2 * D], "uint8"),
    "ps": ("psum", [128, 512 * 8], "float32"),
    "ysb": ("sbuf", [128, NT], "float32"),
}
SEMAPHORES = (["ld_xe", "ld_xm", "ld_wa", "ld_wb", "ld_ta", "ld_tb", "q_xe", "q_xm", "q_he", "q_hm", "q_hr",
               "halo_r", "halo_l", "left", "ya", "yb", "yc", "c_a", "c_b", "c_c", "stored"]
              + ["q_w%d" % i for i in range(4)] + ["q_t%d" % t for t in range(3)]
              + [k + "%d" % b for k in ("ze", "zm", "zr", "ae", "am", "ar") for b in range(4)])
BE, BM, BR = (0, 1, 2, 3), (4, 5, 6, 7), (0, 1, 2, 3)
BA, BB, BC = 4, 5, 6


def rank_program(g, core, T, topo):
    rank = T.rank_of(core)
    if rank is None:
        return
    S = T.sem
    V, P, A, Y = g.vector, g.tensor, g.scalar, g.sync
    n = len(T.cores)
    left, right = T.cores[(rank - 1) % n], T.cores[(rank + 1) % n]
    u8 = dt.uint8
    Relu, Copy = ActivationFunctionType.Relu, ActivationFunctionType.Copy

    def bank(k, a, b):
        return T.ps[:, 512 * k + a:512 * k + b]

    def w1(i):
        return T.w1q[:, 128 * i:128 * i + 128], T.w1s[:, 128 * i:128 * i + 128]

    def wt(t):
        return T.wtq[:, 128 * t:128 * t + 128], T.wts[:, 128 * t:128 * t + 128]

    def xb(a, b):
        return T.xq[:, D * a:D * b], T.xs[:, D * a:D * b]

    def hb(a, b):
        return T.hq[:, D * a:D * b], T.hs[:, D * a:D * b]

    def mm(out, w, x, start, stop):
        return P.matmul_mx(out, w[0], w[1], x[0], x[1], start, stop)

    Y.dma_start(T.xt[:, E:2 * E], T.x[:, 0:E]).then_inc(S.ld_xe, 16)
    A.dma_start(T.xt[:, 0:E], T.x[:, 5 * E:6 * E]).then_inc(S.ld_xe, 16)
    Y.dma_start(T.w1t[:, 0:1024], T.w1[:, 0:1024]).then_inc(S.ld_wa, 16)
    Y.dma_start(T.w1t[:, 1024:2048], T.w1[:, 1024:2048]).then_inc(S.ld_wb, 16)
    Y.dma_start(T.xt[:, 2 * E:6 * E], T.x[:, E:5 * E]).then_inc(S.ld_xm, 16)
    Y.dma_start(T.wtt[:, 0:1024], T.wt[:, 0:1024]).then_inc(S.ld_ta, 16)
    Y.dma_start(T.wtt[:, 1024:1536], T.wt[:, 1024:1536]).then_inc(S.ld_tb, 16)

    def send(dst, remote_sem, cq, ps, a, b):
        rid, pid, _ = topo.addr(dst)
        m = topo.mask(core, dst)
        for o, i in ((cq[:, D * b:D * b + D].bitcast(u8), cq[:, D * a:D * a + D].bitcast(u8)),
                     (ps[:, D * b:D * b + D], ps[:, D * a:D * a + D])):
            g.remote_dma(out_ap=o, in_ap=i, remote_sem=remote_sem, local_sem=S.left, pid=pid, routing_id=rid,
                         dma_engine_mask=m)
        return 2 * bin(m).count("1")

    g.wait_ge(S.q_xe, 1)
    sent = send(left, S.halo_r, T.xq, T.xs, 5, 6)
    g.wait_ge(S.q_he, 1)
    sent += send(right, S.halo_l, T.hq, T.hs, 6, 0)
    g.wait_ge(S.left, sent)
    from_r = 2 * bin(topo.mask(right, core)).count("1")
    from_l = 2 * bin(topo.mask(left, core)).count("1")

    def to_tile(q, kind, b):
        out, zin = {"e": (T.ht[:, b:2 * E:4], bank(BE[b], 0, 2 * D)),
                    "m": (T.ht[:, 2 * E + b:6 * E:4], bank(BM[b], 0, 4 * D)),
                    "r": (T.rt[:, b:2 * E:4], bank(BR[b], 0, 2 * D))}[kind]
        q.wait_ge(S["z%s%d" % (kind, b)], 1)
        if q is V:
            r = V.tensor_scalar(out, zin, 0.0, SC, AluOpType.max, AluOpType.mult)
        else:
            r = A.activation(out, zin, Relu, scale=SC)
        r.then_inc(S["a%s%d" % (kind, b)], 1)

    def wait_tile(kind):
        for b in range(4):
            V.wait_ge(S["a%s%d" % (kind, b)], 1)

    def q_wt(t):
        q, s = wt(t)
        V.quantize_mx(q, s, T.wtt[:, 512 * t:512 * t + 512]).then_inc(S["q_t%d" % t], 1)

    V.wait_ge(S.ld_xe, 32)
    V.quantize_mx(T.xq[:, 4 * D:6 * D], T.xs[:, 4 * D:6 * D], T.xt[:, 0:2 * E]).then_inc(S.q_xe, 1)
    for i in range(4):
        if i == 0:
            V.wait_ge(S.ld_wa, 16)
        if i == 2:
            V.wait_ge(S.ld_wb, 16)
        q, s = w1(i)
        V.quantize_mx(q, s, T.w1t[:, 512 * i:512 * i + 512]).then_inc(S["q_w%d" % i], 1)
    V.wait_ge(S.ld_xm, 16)
    V.quantize_mx(T.xq[:, 0:4 * D], T.xs[:, 0:4 * D], T.xt[:, 2 * E:6 * E]).then_inc(S.q_xm, 1)
    wait_tile("e")
    V.quantize_mx(T.hq[:, 6 * D:8 * D], T.hs[:, 6 * D:8 * D], T.ht[:, 0:2 * E]).then_inc(S.q_he, 1)
    to_tile(V, "m", 1)
    V.wait_ge(S.ld_ta, 16)
    q_wt(1)
    to_tile(V, "m", 3)
    wait_tile("m")
    V.quantize_mx(T.hq[:, D:6 * D], T.hs[:, D:6 * D], T.ht[:, E:6 * E]).then_inc(S.q_hm, 1)
    q_wt(0)
    V.wait_ge(S.ld_tb, 16)
    q_wt(2)
    V.wait_ge(S.yb, 1)
    V.tensor_copy(T.ysb[:, 2 * D:5 * D], bank(BB, 0, 3 * D)).then_inc(S.c_b, 1)
    to_tile(V, "r", 1)
    to_tile(V, "r", 3)
    wait_tile("r")
    V.quantize_mx(T.rq[:], T.rs[:], T.rt[:]).then_inc(S.q_hr, 1)
    V.wait_ge(S.yc, 1)
    V.tensor_copy(T.ysb[:, 5 * D:6 * D], bank(BC, D, 2 * D)).then_inc(S.c_c, 1)

    P.wait_ge(S.q_xe, 1)
    for b in range(4):
        P.wait_ge(S["q_w%d" % b], 1)
        mm(bank(BE[b], 0, 2 * D), w1(b), xb(4, 6), True, True).then_inc(S["ze%d" % b], 1)
    P.wait_ge(S.q_xm, 1)
    for b in (1, 0, 2, 3):
        mm(bank(BM[b], 0, 4 * D), w1(b), xb(0, 4), True, True).then_inc(S["zm%d" % b], 1)
    P.wait_ge(S.q_he, 1)
    P.wait_ge(S.q_hm, 1)
    P.wait_ge(S.q_t1, 1)
    mm(bank(BA, 0, 2 * D), wt(1), hb(1, 3), True, False)
    mm(bank(BB, 0, 3 * D), wt(1), hb(3, 6), True, False)
    P.wait_ge(S.q_t0, 1)
    mm(bank(BB, 0, 3 * D), wt(0), hb(2, 5), False, False)
    P.wait_ge(S.q_t2, 1)
    mm(bank(BB, 0, 3 * D), wt(2), hb(4, 7), False, True).then_inc(S.yb, 1)
    P.wait_ge(S.halo_r, from_r)
    for b in range(4):
        mm(bank(BR[b], 0, 2 * D), w1(b), xb(5, 7), True, True).then_inc(S["zr%d" % b], 1)
    mm(bank(BA, 0, 2 * D), wt(2), hb(2, 4), False, False)
    mm(bank(BC, 0, 2 * D), wt(0), hb(4, 6), True, False)
    P.wait_ge(S.halo_l, from_l)
    mm(bank(BA, 0, 2 * D), wt(0), hb(0, 2), False, True).then_inc(S.ya, 1)
    mm(bank(BC, 0, 2 * D), wt(1), hb(5, 7), False, False)
    P.wait_ge(S.q_hr, 1)
    mm(bank(BC, 0, 2 * D), wt(2), (T.rq[:], T.rs[:]), False, True).then_inc(S.yc, 1)

    for b in range(4):
        to_tile(A, "e", b)
    for b in (0, 2):
        to_tile(A, "m", b)
    for b in (0, 2):
        to_tile(A, "r", b)
    A.wait_ge(S.ya, 1)
    A.activation(T.ysb[:, 0:2 * D], bank(BA, 0, 2 * D), Copy).then_inc(S.c_a, 1)
    A.wait_ge(S.c_a, 1)
    A.dma_start(T.y[:, 0:2 * D], T.ysb[:, 0:2 * D]).then_inc(S.stored, 16)

    Y.wait_ge(S.c_b, 1)
    Y.dma_start(T.y[:, 2 * D:5 * D], T.ysb[:, 2 * D:5 * D]).then_inc(S.stored, 16)
    Y.wait_ge(S.c_c, 1)
    Y.dma_start(T.y[:, 5 * D:6 * D], T.ysb[:, 5 * D:6 * D]).then_inc(S.stored, 16)
    Y.wait_ge(S.stored, 48)
